import numpy as np
import ml_dtypes


def mxq(x, axis, fmt="e4m3"):
    dtype, down = {"e4m3": (ml_dtypes.float8_e4m3fn, 7), "e5m2": (ml_dtypes.float8_e5m2, 14)}[fmt]
    v = np.moveaxis(np.asarray(x, np.float32).astype(ml_dtypes.bfloat16).astype(np.float64), axis, -1)
    blocks = v.reshape(v.shape[:-1] + (-1, 32))
    amax = np.abs(blocks).max(-1, keepdims=True)
    byte = np.maximum(np.where(amax > 0, np.frexp(amax)[1] - 1 + 127, 0) - down, 1)
    scale = np.exp2(byte - 127.0)
    codes = (blocks / scale).astype(np.float32).astype(dtype).astype(np.float64)
    return np.moveaxis((codes * scale).reshape(v.shape), -1, axis)


WIDE = False


def mx_kscale(k):
    if not WIDE:
        return np.ones(k)
    levels = np.array([10, -10, 5, -5, 0])
    if k % 512:
        return np.exp2(np.random.permutation(np.resize(levels, k // 32))).repeat(32)
    a = np.empty((k // 512, 16))
    for p in range(k // 512):
        a[p, :8] = np.random.permutation(np.resize(levels, 8))
        for g in range(8):
            far = levels[np.abs(levels - a[p, g]) >= 10]
            a[p, g + 8] = far[np.random.randint(len(far))]
    return np.exp2(a.ravel()).repeat(32)


def f64(x):
    return np.asarray(x).astype(np.float64)


def striped(idx):
    return np.tile(idx.reshape(-1, 16).T, (8, 1)).astype(np.uint16)


def unstriped(offs):
    return offs[:16].T.reshape(-1).astype(np.int64)


def striped8(idx):
    return np.concatenate([x.reshape(-1, 16).T for x in idx]).astype(np.uint16)


def runs(offs, k):
    lists = np.stack([offs[16 * r : 16 * r + 16].T.reshape(-1) for r in range(8)]).astype(np.int64)
    return lists[np.arange(k) % 512 // 64]


def pack_weight(w):
    k, n = w.shape
    w = f64(np.asarray(w, np.float32).astype(ml_dtypes.bfloat16)).reshape(k // 32, 32, n)
    amax = np.abs(w).max(1)
    byte = np.clip(np.where(amax > 0, np.frexp(amax)[1] - 1 + 127 - 7, 1), 1, 254)
    scaled = (w * np.exp2(127.0 - byte)[:, None, :]).reshape(k, n).astype(np.float32)
    words = np.ascontiguousarray(scaled.reshape(k // 512, 128, 4, n).transpose(0, 1, 3, 2)).astype(ml_dtypes.float8_e4m3fn).view(np.uint8)
    return words, np.ascontiguousarray(byte.astype(np.uint8).reshape(k // 512, 16, n))


def unpack_weight(words, scales):
    g, p, n, _ = words.shape
    vals = np.ascontiguousarray(words).view(ml_dtypes.float8_e4m3fn).astype(np.float64) * np.repeat(np.exp2(scales.astype(np.float64) - 127.0), 8, axis=1)[..., None]
    return vals.transpose(0, 1, 3, 2).reshape(g * 512, n)


K, T, S, H, C, W = 512, 2048, 512, 512, 512, 256


def setup_inputs():
    n = np.random.standard_normal
    s = mx_kscale(K)[:, None]
    packed_xT = pack_weight(n((K, T)) * s)
    perm = np.stack([np.random.permutation(S) for _ in range(8)])
    return {
        "x_words": packed_xT[0],
        "x_scales": packed_xT[1],
        "w1": (n((K, H)) / np.sqrt(2 * K) / s).astype(np.float32),
        "w2": (n((K, H)) / np.sqrt(2 * K) / s).astype(np.float32),
        "gs": (np.random.uniform(0.5, 1.5, (K, 1)) / s).astype(np.float32),
        "offs": striped(np.random.permutation(T)[:S]),
        "hz": striped8(np.random.randint(0, T, (8, S))),
        "cand": striped(np.random.permutation(T)[:C]),
        "n1": striped8(perm[:, :W]),
        "n2": striped8(perm[:, W:]),
    }


def reference(x_words, x_scales, w1, w2, gs, offs, hz, cand, n1, n2):
    x_cand = unpack_weight(x_words, x_scales)[:, unstriped(cand)]
    xq = unpack_weight(x_words, x_scales)[:, unstriped(offs)]
    x_hz = unpack_weight(x_words, x_scales)[np.arange(K)[:, None], runs(hz, K)]
    y = mxq(f64(w1), 0, "e4m3").T @ xq + mxq(f64(w2), 0, "e4m3").T @ x_hz
    z = f64(gs) * y
    s = 0.0625 * ((x_cand.T @ mxq(z, 0, "e4m3")))
    pa = s[np.arange(C)[:, None], runs(n1, C)]
    pb = s[np.arange(C)[:, None], runs(n2, C)]
    ra = np.maximum(pa, pb)
    out = s.copy()
    out[np.arange(C)[:, None], runs(n1, C)] = ra
    return out

@@ -1,0 +1,185 @@
+from contextlib import ExitStack
+
+import concourse.mybir as mybir
+
+K, T, S, H, C, W = 512, 2048, 512, 512, 512, 256
+FLOPS = 3 * 2 * 512 * 512 * 512
+
+F32 = mybir.dt.float32
+BF16 = mybir.dt.bfloat16
+I32 = mybir.dt.int32
+U32 = mybir.dt.uint32
+U16 = mybir.dt.uint16
+U8 = mybir.dt.uint8
+FP8X4 = mybir.dt.float8_e4m3fn_x4
+COPY = mybir.ActivationFunctionType.Copy
+ALU = mybir.AluOpType
+
+P = 128
+PACK = 4
+CHUNK = 128
+CHUNKS = S // CHUNK
+HALF = P // 2
+
+
+def tile_picked_thcifill_none_p_kernel(
+    tc, x_words, x_scales, w1, w2, gs, offs, hz, cand, n1, n2, out
+):
+    nc = tc.nc
+    with ExitStack() as ctx:
+        lists = ctx.enter_context(tc.tile_pool(name="lists", bufs=1))
+        keep = ctx.enter_context(tc.tile_pool(name="keep", bufs=1))
+        psum = ctx.enter_context(tc.psum_pool(name="psum", bufs=1))
+
+        hz_list = lists.tile([P, S // 16], U16, name="hz_list")
+        offs_list = lists.tile([P, S // 16], U16, name="offs_list")
+        cand_list = lists.tile([P, C // 16], U16, name="cand_list")
+        n1_list = lists.tile([P, W // 16], U16, name="n1_list")
+        n2_list = lists.tile([P, W // 16], U16, name="n2_list")
+
+        byte_table = keep.tile([P, T], U8, name="byte_table")
+        word_table = keep.tile([P, T], I32, name="word_table")
+        raw = [[keep.tile([P, PACK, H // 2], F32, name=f"w{n}_raw{h}") for h in range(2)] for n in range(2)]
+        gains = keep.tile([P, PACK], F32, name="gains")
+        picked_bytes = keep.tile([P, 3, S], U8, name="picked_bytes")
+        planes = keep.tile([P, 3, S], U8, name="planes", align_bytes=64)
+        planes_words = planes[:].rearrange("p l s -> p (l s)").bitcast(I32)
+        picked_bytes_words = picked_bytes[:].rearrange("p l s -> p (l s)").bitcast(I32)
+
+        def load_weight(n, h):
+            rows = (w1, w2)[n].rearrange("(p j) c -> p j c", j=PACK)
+            nc.sync.dma_start(out=raw[n][h][:], in_=rows[:, :, h * (H // 2) : (h + 1) * (H // 2)])
+
+        nc.sync.dma_start(
+            out=byte_table[:].bitcast(I32),
+            in_=x_scales[0].bitcast(I32).unsqueeze(1).to_broadcast([16, 8, T // 4]),
+        )
+        nc.vector.memset(planes_words, 0)
+        nc.sync.dma_start(hz_list[:], hz)
+        nc.sync.dma_start(offs_list[:], offs)
+        load_weight(0, 0)
+        nc.sync.dma_start(cand_list[:], cand)
+        nc.sync.dma_start(out=word_table[:], in_=x_words[0].rearrange("p c r -> p (c r)").bitcast(I32))
+        load_weight(0, 1)
+        load_weight(1, 0)
+        load_weight(1, 1)
+        nc.gpsimd.dma_start(out=gains[:], in_=gs.rearrange("(p t) o -> p (t o)", t=PACK))
+        nc.sync.dma_start(n1_list[:], n1)
+        nc.sync.dma_start(n2_list[:], n2)
+
+        codes = [keep.tile([P, H], U32, name=f"w{n}_codes", align_bytes=64) for n in range(2)]
+        plane = [keep.tile([P, H], U8, name=f"w{n}_plane", align_bytes=64) for n in range(2)]
+        rounded = [[keep.tile([P, PACK, HALF, PACK], BF16, name=f"w{n}_bf{h}", align_bytes=64) for h in range(2)] for n in range(2)]
+
+        def round_weight(n, h):
+            nc.scalar.copy(
+                out=rounded[n][h][:].rearrange("p t m j -> p m t j"),
+                in_=raw[n][h][:].rearrange("p j (m t) -> p m t j", t=PACK),
+            )
+
+        def quantize_weight(n, h):
+            for t in range(PACK):
+                cols = slice(t * P + h * HALF, t * P + (h + 1) * HALF)
+                nc.vector.quantize_mx(
+                    out=codes[n][:, cols].bitcast(FP8X4),
+                    scales=plane[n][:, cols],
+                    in_=rounded[n][h][:, t, :, :].rearrange("p m j -> p (m j)"),
+                )
+
+        round_weight(0, 0)
+        nc.vector.tensor_copy(picked_bytes[:, 0, :], byte_table[:].indirect(hz_list[:]))
+        nc.vector.tensor_copy(picked_bytes[:, 1, :], byte_table[:].indirect(offs_list[:]))
+        nc.vector.tensor_copy(
+            picked_bytes[:, 2, :].rearrange("p (t m) -> p m t", t=PACK), byte_table[:].indirect(cand_list[:])
+        )
+        for r in range(4):
+            nc.scalar.dma_start(out=planes_words[r:P:32, :], in_=picked_bytes_words[8 * r : P : 32, :])
+        round_weight(0, 1)
+        round_weight(1, 0)
+        round_weight(1, 1)
+
+        offs_words = keep.tile([P, S], U32, name="offs_words", align_bytes=64)
+        hz_words = keep.tile([P, S], U32, name="hz_words", align_bytes=64)
+        cand_words = keep.tile([P, C], U32, name="cand_words", align_bytes=64)
+        word_window = word_table[:].bitcast(U32)
+        quantize_weight(0, 0)
+        nc.vector.tensor_copy(offs_words[:], word_window.indirect(offs_list[:]))
+        nc.vector.tensor_copy(hz_words[:], word_window.indirect(hz_list[:]))
+        quantize_weight(0, 1)
+        nc.vector.tensor_copy(
+            cand_words[:].rearrange("p (t m) -> p m t", t=PACK), word_window.indirect(cand_list[:])
+        )
+        quantize_weight(1, 0)
+        quantize_weight(1, 1)
+
+        y_banks = [psum.tile([P, PACK, CHUNK], F32, name=f"y_bank{b}") for b in range(CHUNKS)]
+        for first, n, words, which in ((True, 0, offs_words, 1), (False, 1, hz_words, 0)):
+            for b in range(CHUNKS):
+                cols = slice(b * CHUNK, (b + 1) * CHUNK)
+                for t in range(PACK):
+                    rows = slice(t * P, (t + 1) * P)
+                    nc.tensor.matmul_mx(
+                        out=y_banks[b][:, t, :],
+                        lhsT=codes[n][:, rows].bitcast(FP8X4),
+                        lhsT_scale=plane[n][:, rows],
+                        rhs=words[:, cols].bitcast(FP8X4),
+                        rhs_scale=planes[:, which, cols],
+                        start=(first and t == 0),
+                        stop=((not first) and t == PACK - 1),
+                    )
+
+        z_codes = keep.tile([P, S], U32, name="z_codes", align_bytes=64)
+        z_plane = keep.tile([P, S], U8, name="z_plane", align_bytes=64)
+        s_banks = [psum.tile([P, PACK, CHUNK], F32, name=f"s_bank{b}") for b in range(CHUNKS)]
+        s_tiles = [keep.tile([P, S], F32, name=f"s_tile{t}") for t in range(PACK)]
+        z_bf = [keep.tile([P, CHUNK, PACK], BF16, name=f"z_bf{b}", align_bytes=64) for b in range(CHUNKS)]
+
+        def weigh(b):
+            nc.vector.tensor_tensor(
+                out=z_bf[b][:],
+                in0=y_banks[b][:].rearrange("p t n -> p n t"),
+                in1=gains[:].unsqueeze(1).to_broadcast([P, CHUNK, PACK]),
+                op=ALU.mult,
+            )
+
+        def score(b):
+            cols = slice(b * CHUNK, (b + 1) * CHUNK)
+            nc.vector.quantize_mx(
+                out=z_codes[:, cols].bitcast(FP8X4),
+                scales=z_plane[:, cols],
+                in_=z_bf[b][:].rearrange("p n t -> p (n t)"),
+            )
+            for t in range(PACK):
+                rows = slice(t * P, (t + 1) * P)
+                nc.tensor.matmul_mx(
+                    out=s_banks[b][:, t, :],
+                    lhsT=cand_words[:, rows].bitcast(FP8X4),
+                    lhsT_scale=planes[:, 2, rows],
+                    rhs=z_codes[:, cols].bitcast(FP8X4),
+                    rhs_scale=z_plane[:, cols],
+                    start=True,
+                    stop=True,
+                )
+            for t in range(PACK):
+                nc.scalar.activation(out=s_tiles[t][:, cols], in_=s_banks[b][:, t, :], func=COPY, scale=0.0625)
+
+        weigh(0)
+        for b in range(1, CHUNKS):
+            weigh(b)
+            score(b - 1)
+        score(CHUNKS - 1)
+
+        out_rows = out.rearrange("(p t) j -> p t j", t=PACK)
+        for t in range(PACK):
+            s_tile = s_tiles[t]
+            pa = keep.tile([P, W], F32, name=f"pa{t}")
+            pb = keep.tile([P, W], F32, name=f"pb{t}")
+            ra = keep.tile([P, W], F32, name=f"ra{t}")
+            nc.scalar.activation(out=pb[:], in_=s_tile[:].indirect(n2_list[:]), func=COPY)
+            if t == 0:
+                nc.vector.tensor_copy(pa[:], s_tile[:].indirect(n1_list[:]))
+            else:
+                nc.scalar.activation(out=pa[:], in_=s_tile[:].indirect(n1_list[:]), func=COPY)
+            nc.vector.tensor_tensor(out=ra[:], in0=pa[:], in1=pb[:], op=ALU.max)
+            nc.vector.tensor_copy(s_tile[:].indirect(n1_list[:]), ra[:])
+            nc.sync.dma_start(out=out_rows[:, t, :], in_=s_tile[:])

@@ -39,7 +39,7 @@ def tile_picked_thcifill_none_p_kernel(
 
         byte_table = keep.tile([P, T], U8, name="byte_table")
         word_table = keep.tile([P, T], I32, name="word_table")
-        raw = [[keep.tile([P, PACK, H // 2], F32, name=f"w{n}_raw{h}") for h in range(2)] for n in range(2)]
+        raw = {}
         gains = keep.tile([P, PACK], F32, name="gains")
         picked_bytes = keep.tile([P, 3, S], U8, name="picked_bytes")
         planes = keep.tile([P, 3, S], U8, name="planes", align_bytes=64)
@@ -47,8 +47,10 @@ def tile_picked_thcifill_none_p_kernel(
         picked_bytes_words = picked_bytes[:].rearrange("p l s -> p (l s)").bitcast(I32)
 
         def load_weight(n, h):
+            slot = (2 * n + h) % 3
+            raw[n, h] = keep.tile([P, PACK, H // 2], F32, name=f"w{n}_raw{h}", tag=f"raw{slot}")
             rows = (w1, w2)[n].rearrange("(p j) c -> p j c", j=PACK)
-            nc.sync.dma_start(out=raw[n][h][:], in_=rows[:, :, h * (H // 2) : (h + 1) * (H // 2)])
+            nc.sync.dma_start(out=raw[n, h][:], in_=rows[:, :, h * (H // 2) : (h + 1) * (H // 2)])
 
         nc.sync.dma_start(
             out=byte_table[:].bitcast(I32),
@@ -59,41 +61,39 @@ def tile_picked_thcifill_none_p_kernel(
         nc.sync.dma_start(offs_list[:], offs)
         load_weight(0, 0)
         nc.sync.dma_start(cand_list[:], cand)
-        nc.sync.dma_start(out=word_table[:], in_=x_words[0].rearrange("p c r -> p (c r)").bitcast(I32))
         load_weight(0, 1)
+        nc.sync.dma_start(out=word_table[:], in_=x_words[0].rearrange("p c r -> p (c r)").bitcast(I32))
         load_weight(1, 0)
-        load_weight(1, 1)
         nc.gpsimd.dma_start(out=gains[:], in_=gs.rearrange("(p t) o -> p (t o)", t=PACK))
         nc.sync.dma_start(n1_list[:], n1)
         nc.sync.dma_start(n2_list[:], n2)
 
         codes = [keep.tile([P, H], U32, name=f"w{n}_codes", align_bytes=64) for n in range(2)]
         plane = [keep.tile([P, H], U8, name=f"w{n}_plane", align_bytes=64) for n in range(2)]
-        rounded = [[keep.tile([P, PACK, HALF, PACK], BF16, name=f"w{n}_bf{h}", align_bytes=64) for h in range(2)] for n in range(2)]
+        rounded = [keep.tile([P, PACK, P, PACK], BF16, name=f"w{n}_bf", align_bytes=64) for n in range(2)]
 
         def round_weight(n, h):
             nc.scalar.copy(
-                out=rounded[n][h][:].rearrange("p t m j -> p m t j"),
-                in_=raw[n][h][:].rearrange("p j (m t) -> p m t j", t=PACK),
+                out=rounded[n][:, :, h * HALF : (h + 1) * HALF, :].rearrange("p (u v) m j -> p m u j v", v=2),
+                in_=raw[n, h][:].rearrange("p j (m u v) -> p m u j v", u=2, v=2),
             )
 
-        def quantize_weight(n, h):
-            for t in range(PACK):
-                cols = slice(t * P + h * HALF, t * P + (h + 1) * HALF)
-                nc.vector.quantize_mx(
-                    out=codes[n][:, cols].bitcast(FP8X4),
-                    scales=plane[n][:, cols],
-                    in_=rounded[n][h][:, t, :, :].rearrange("p m j -> p (m j)"),
-                )
+        def quantize_weight(n):
+            nc.vector.quantize_mx(
+                out=codes[n][:].bitcast(FP8X4),
+                scales=plane[n][:],
+                in_=rounded[n][:].rearrange("p t m j -> p (t m j)"),
+            )
 
         round_weight(0, 0)
         nc.vector.tensor_copy(picked_bytes[:, 0, :], byte_table[:].indirect(hz_list[:]))
         nc.vector.tensor_copy(picked_bytes[:, 1, :], byte_table[:].indirect(offs_list[:]))
         nc.vector.tensor_copy(
-            picked_bytes[:, 2, :].rearrange("p (t m) -> p m t", t=PACK), byte_table[:].indirect(cand_list[:])
+            picked_bytes[:, 2, :].rearrange("p (t a e) -> p a t e", t=PACK, e=8), byte_table[:].indirect(cand_list[:])
         )
         for r in range(4):
-            nc.scalar.dma_start(out=planes_words[r:P:32, :], in_=picked_bytes_words[8 * r : P : 32, :])
+            nc.sync.dma_start(out=planes_words[r:P:32, :], in_=picked_bytes_words[8 * r : P : 32, :])
+        load_weight(1, 1)
         round_weight(0, 1)
         round_weight(1, 0)
         round_weight(1, 1)
@@ -102,15 +102,13 @@ def tile_picked_thcifill_none_p_kernel(
         hz_words = keep.tile([P, S], U32, name="hz_words", align_bytes=64)
         cand_words = keep.tile([P, C], U32, name="cand_words", align_bytes=64)
         word_window = word_table[:].bitcast(U32)
-        quantize_weight(0, 0)
+        quantize_weight(0)
         nc.vector.tensor_copy(offs_words[:], word_window.indirect(offs_list[:]))
         nc.vector.tensor_copy(hz_words[:], word_window.indirect(hz_list[:]))
-        quantize_weight(0, 1)
         nc.vector.tensor_copy(
-            cand_words[:].rearrange("p (t m) -> p m t", t=PACK), word_window.indirect(cand_list[:])
+            cand_words[:].rearrange("p (t a e) -> p a t e", t=PACK, e=8), word_window.indirect(cand_list[:])
         )
-        quantize_weight(1, 0)
-        quantize_weight(1, 1)
+        quantize_weight(1)
 
         y_banks = [psum.tile([P, PACK, CHUNK], F32, name=f"y_bank{b}") for b in range(CHUNKS)]
         for first, n, words, which in ((True, 0, offs_words, 1), (False, 1, hz_words, 0)):
@@ -149,10 +147,14 @@ def tile_picked_thcifill_none_p_kernel(
                 scales=z_plane[:, cols],
                 in_=z_bf[b][:].rearrange("p n t -> p (n t)"),
             )
+            targets = [s_banks[b][:, t, :] for t in range(PACK)]
+            if b == CHUNKS - 1:
+                lead_bank = psum.tile([P, CHUNK], F32, name="lead_bank", tag="y_bank0")
+                targets[0] = lead_bank[:]
             for t in range(PACK):
                 rows = slice(t * P, (t + 1) * P)
                 nc.tensor.matmul_mx(
-                    out=s_banks[b][:, t, :],
+                    out=targets[t],
                     lhsT=cand_words[:, rows].bitcast(FP8X4),
                     lhsT_scale=planes[:, 2, rows],
                     rhs=z_codes[:, cols].bitcast(FP8X4),
@@ -161,7 +163,12 @@ def tile_picked_thcifill_none_p_kernel(
                     stop=True,
                 )
             for t in range(PACK):
-                nc.scalar.activation(out=s_tiles[t][:, cols], in_=s_banks[b][:, t, :], func=COPY, scale=0.0625)
+                if b == CHUNKS - 1 and t == 0:
+                    nc.vector.tensor_scalar(
+                        out=s_tiles[t][:, cols], in0=targets[t], scalar1=0.0625, scalar2=None, op0=ALU.mult
+                    )
+                else:
+                    nc.scalar.activation(out=s_tiles[t][:, cols], in_=targets[t], func=COPY, scale=0.0625)
 
         weigh(0)
         for b in range(1, CHUNKS):
@@ -169,17 +176,18 @@ def tile_picked_thcifill_none_p_kernel(
             score(b - 1)
         score(CHUNKS - 1)
 
-        out_rows = out.rearrange("(p t) j -> p t j", t=PACK)
-        for t in range(PACK):
-            s_tile = s_tiles[t]
-            pa = keep.tile([P, W], F32, name=f"pa{t}")
-            pb = keep.tile([P, W], F32, name=f"pb{t}")
-            ra = keep.tile([P, W], F32, name=f"ra{t}")
-            nc.scalar.activation(out=pb[:], in_=s_tile[:].indirect(n2_list[:]), func=COPY)
-            if t == 0:
-                nc.vector.tensor_copy(pa[:], s_tile[:].indirect(n1_list[:]))
-            else:
-                nc.scalar.activation(out=pa[:], in_=s_tile[:].indirect(n1_list[:]), func=COPY)
+        out_rows = out.rearrange("(a t e) j -> t a e j", t=PACK, e=8)
+        for group in ((0,), (1,), (2, 3)):
+            pa = keep.tile([P, len(group), W], F32, name=f"pa{group[0]}")
+            pb = keep.tile([P, len(group), W], F32, name=f"pb{group[0]}")
+            ra = keep.tile([P, len(group), W], F32, name=f"ra{group[0]}")
+            for i, t in enumerate(group):
+                nc.scalar.activation(out=pb[:, i, :], in_=s_tiles[t][:].indirect(n2_list[:]), func=COPY)
+                if t == 0:
+                    nc.vector.tensor_copy(pa[:, i, :], s_tiles[t][:].indirect(n1_list[:]))
+                else:
+                    nc.scalar.activation(out=pa[:, i, :], in_=s_tiles[t][:].indirect(n1_list[:]), func=COPY)
             nc.vector.tensor_tensor(out=ra[:], in0=pa[:], in1=pb[:], op=ALU.max)
-            nc.vector.tensor_copy(s_tile[:].indirect(n1_list[:]), ra[:])
-            nc.sync.dma_start(out=out_rows[:, t, :], in_=s_tile[:])
+            for i, t in enumerate(group):
+                nc.vector.tensor_copy(s_tiles[t][:].indirect(n1_list[:]), ra[:, i, :])
+                nc.sync.dma_start(out=out_rows[t], in_=s_tiles[t][:])

from contextlib import ExitStack

import concourse.mybir as mybir

K, T, S, H, C, W = 512, 2048, 512, 512, 512, 256
FLOPS = 3 * 2 * 512 * 512 * 512

F32 = mybir.dt.float32
BF16 = mybir.dt.bfloat16
I32 = mybir.dt.int32
U32 = mybir.dt.uint32
U16 = mybir.dt.uint16
U8 = mybir.dt.uint8
FP8X4 = mybir.dt.float8_e4m3fn_x4
COPY = mybir.ActivationFunctionType.Copy
ALU = mybir.AluOpType

P = 128
PACK = 4
CHUNK = 128
CHUNKS = S // CHUNK
HALF = P // 2


def tile_picked_thcifill_none_p_kernel(
    tc, x_words, x_scales, w1, w2, gs, offs, hz, cand, n1, n2, out
):
    nc = tc.nc
    with ExitStack() as ctx:
        lists = ctx.enter_context(tc.tile_pool(name="lists", bufs=1))
        keep = ctx.enter_context(tc.tile_pool(name="keep", bufs=1))
        psum = ctx.enter_context(tc.psum_pool(name="psum", bufs=1))

        hz_list = lists.tile([P, S // 16], U16, name="hz_list")
        offs_list = lists.tile([P, S // 16], U16, name="offs_list")
        cand_list = lists.tile([P, C // 16], U16, name="cand_list")
        n1_list = lists.tile([P, W // 16], U16, name="n1_list")
        n2_list = lists.tile([P, W // 16], U16, name="n2_list")

        byte_table = keep.tile([P, T], U8, name="byte_table")
        word_table = keep.tile([P, T], I32, name="word_table")
        raw = {}
        gains = keep.tile([P, PACK], F32, name="gains")
        picked_bytes = keep.tile([P, 3, S], U8, name="picked_bytes")
        planes = keep.tile([P, 3, S], U8, name="planes", align_bytes=64)
        planes_words = planes[:].rearrange("p l s -> p (l s)").bitcast(I32)
        picked_bytes_words = picked_bytes[:].rearrange("p l s -> p (l s)").bitcast(I32)

        def load_weight(n, h):
            slot = (2 * n + h) % 3
            raw[n, h] = keep.tile([P, PACK, H // 2], F32, name=f"w{n}_raw{h}", tag=f"raw{slot}")
            rows = (w1, w2)[n].rearrange("(p j) c -> p j c", j=PACK)
            nc.sync.dma_start(out=raw[n, h][:], in_=rows[:, :, h * (H // 2) : (h + 1) * (H // 2)])

        nc.sync.dma_start(
            out=byte_table[:].bitcast(I32),
            in_=x_scales[0].bitcast(I32).unsqueeze(1).to_broadcast([16, 8, T // 4]),
        )
        nc.vector.memset(planes_words, 0)
        nc.sync.dma_start(hz_list[:], hz)
        nc.sync.dma_start(offs_list[:], offs)
        load_weight(0, 0)
        nc.sync.dma_start(cand_list[:], cand)
        load_weight(0, 1)
        nc.sync.dma_start(out=word_table[:], in_=x_words[0].rearrange("p c r -> p (c r)").bitcast(I32))
        load_weight(1, 0)
        nc.gpsimd.dma_start(out=gains[:], in_=gs.rearrange("(p t) o -> p (t o)", t=PACK))
        nc.sync.dma_start(n1_list[:], n1)
        nc.sync.dma_start(n2_list[:], n2)

        codes = [keep.tile([P, H], U32, name=f"w{n}_codes", align_bytes=64) for n in range(2)]
        plane = [keep.tile([P, H], U8, name=f"w{n}_plane", align_bytes=64) for n in range(2)]
        rounded = [keep.tile([P, PACK, P, PACK], BF16, name=f"w{n}_bf", align_bytes=64) for n in range(2)]

        def round_weight(n, h):
            nc.scalar.copy(
                out=rounded[n][:, :, h * HALF : (h + 1) * HALF, :].rearrange("p (u v) m j -> p m u j v", v=2),
                in_=raw[n, h][:].rearrange("p j (m u v) -> p m u j v", u=2, v=2),
            )

        def quantize_weight(n):
            nc.vector.quantize_mx(
                out=codes[n][:].bitcast(FP8X4),
                scales=plane[n][:],
                in_=rounded[n][:].rearrange("p t m j -> p (t m j)"),
            )

        round_weight(0, 0)
        nc.vector.tensor_copy(picked_bytes[:, 0, :], byte_table[:].indirect(hz_list[:]))
        nc.vector.tensor_copy(picked_bytes[:, 1, :], byte_table[:].indirect(offs_list[:]))
        nc.vector.tensor_copy(
            picked_bytes[:, 2, :].rearrange("p (t a e) -> p a t e", t=PACK, e=8), byte_table[:].indirect(cand_list[:])
        )
        for r in range(4):
            nc.sync.dma_start(out=planes_words[r:P:32, :], in_=picked_bytes_words[8 * r : P : 32, :])
        load_weight(1, 1)
        round_weight(0, 1)
        round_weight(1, 0)
        round_weight(1, 1)

        offs_words = keep.tile([P, S], U32, name="offs_words", align_bytes=64)
        hz_words = keep.tile([P, S], U32, name="hz_words", align_bytes=64)
        cand_words = keep.tile([P, C], U32, name="cand_words", align_bytes=64)
        word_window = word_table[:].bitcast(U32)
        quantize_weight(0)
        nc.vector.tensor_copy(offs_words[:], word_window.indirect(offs_list[:]))
        nc.vector.tensor_copy(hz_words[:], word_window.indirect(hz_list[:]))
        nc.vector.tensor_copy(
            cand_words[:].rearrange("p (t a e) -> p a t e", t=PACK, e=8), word_window.indirect(cand_list[:])
        )
        quantize_weight(1)

        y_banks = [psum.tile([P, PACK, CHUNK], F32, name=f"y_bank{b}") for b in range(CHUNKS)]
        for first, n, words, which in ((True, 0, offs_words, 1), (False, 1, hz_words, 0)):
            for b in range(CHUNKS):
                cols = slice(b * CHUNK, (b + 1) * CHUNK)
                for t in range(PACK):
                    rows = slice(t * P, (t + 1) * P)
                    nc.tensor.matmul_mx(
                        out=y_banks[b][:, t, :],
                        lhsT=codes[n][:, rows].bitcast(FP8X4),
                        lhsT_scale=plane[n][:, rows],
                        rhs=words[:, cols].bitcast(FP8X4),
                        rhs_scale=planes[:, which, cols],
                        start=(first and t == 0),
                        stop=((not first) and t == PACK - 1),
                    )

        z_codes = keep.tile([P, S], U32, name="z_codes", align_bytes=64)
        z_plane = keep.tile([P, S], U8, name="z_plane", align_bytes=64)
        s_banks = [psum.tile([P, PACK, CHUNK], F32, name=f"s_bank{b}") for b in range(CHUNKS)]
        s_tiles = [keep.tile([P, S], F32, name=f"s_tile{t}") for t in range(PACK)]
        z_bf = [keep.tile([P, CHUNK, PACK], BF16, name=f"z_bf{b}", align_bytes=64) for b in range(CHUNKS)]

        def weigh(b):
            nc.vector.tensor_tensor(
                out=z_bf[b][:],
                in0=y_banks[b][:].rearrange("p t n -> p n t"),
                in1=gains[:].unsqueeze(1).to_broadcast([P, CHUNK, PACK]),
                op=ALU.mult,
            )

        def score(b):
            cols = slice(b * CHUNK, (b + 1) * CHUNK)
            nc.vector.quantize_mx(
                out=z_codes[:, cols].bitcast(FP8X4),
                scales=z_plane[:, cols],
                in_=z_bf[b][:].rearrange("p n t -> p (n t)"),
            )
            targets = [s_banks[b][:, t, :] for t in range(PACK)]
            if b == CHUNKS - 1:
                lead_bank = psum.tile([P, CHUNK], F32, name="lead_bank", tag="y_bank0")
                targets[0] = lead_bank[:]
            for t in range(PACK):
                rows = slice(t * P, (t + 1) * P)
                nc.tensor.matmul_mx(
                    out=targets[t],
                    lhsT=cand_words[:, rows].bitcast(FP8X4),
                    lhsT_scale=planes[:, 2, rows],
                    rhs=z_codes[:, cols].bitcast(FP8X4),
                    rhs_scale=z_plane[:, cols],
                    start=True,
                    stop=True,
                )
            for t in range(PACK):
                if b == CHUNKS - 1 and t == 0:
                    nc.vector.tensor_scalar(
                        out=s_tiles[t][:, cols], in0=targets[t], scalar1=0.0625, scalar2=None, op0=ALU.mult
                    )
                else:
                    nc.scalar.activation(out=s_tiles[t][:, cols], in_=targets[t], func=COPY, scale=0.0625)

        weigh(0)
        for b in range(1, CHUNKS):
            weigh(b)
            score(b - 1)
        score(CHUNKS - 1)

        out_rows = out.rearrange("(a t e) j -> t a e j", t=PACK, e=8)
        for group in ((0,), (1,), (2, 3)):
            pa = keep.tile([P, len(group), W], F32, name=f"pa{group[0]}")
            pb = keep.tile([P, len(group), W], F32, name=f"pb{group[0]}")
            ra = keep.tile([P, len(group), W], F32, name=f"ra{group[0]}")
            for i, t in enumerate(group):
                nc.scalar.activation(out=pb[:, i, :], in_=s_tiles[t][:].indirect(n2_list[:]), func=COPY)
                if t == 0:
                    nc.vector.tensor_copy(pa[:, i, :], s_tiles[t][:].indirect(n1_list[:]))
                else:
                    nc.scalar.activation(out=pa[:, i, :], in_=s_tiles[t][:].indirect(n1_list[:]), func=COPY)
            nc.vector.tensor_tensor(out=ra[:], in0=pa[:], in1=pb[:], op=ALU.max)
            for i, t in enumerate(group):
                nc.vector.tensor_copy(s_tiles[t][:].indirect(n1_list[:]), ra[:, i, :])
                nc.sync.dma_start(out=out_rows[t], in_=s_tiles[t][:])
